import numpy as np
import ml_dtypes


def mxq(x, axis, fmt="e4m3"):
    dtype, down = {"e4m3": (ml_dtypes.float8_e4m3fn, 7), "e5m2": (ml_dtypes.float8_e5m2, 14)}[fmt]
    v = np.moveaxis(np.asarray(x, np.float32).astype(ml_dtypes.bfloat16).astype(np.float64), axis, -1)
    blocks = v.reshape(v.shape[:-1] + (-1, 32))
    amax = np.abs(blocks).max(-1, keepdims=True)
    byte = np.maximum(np.where(amax > 0, np.frexp(amax)[1] - 1 + 127, 0) - down, 1)
    scale = np.exp2(byte - 127.0)
    codes = (blocks / scale).astype(np.float32).astype(dtype).astype(np.float64)
    return np.moveaxis((codes * scale).reshape(v.shape), -1, axis)


WIDE = False


def mx_kscale(k):
    if not WIDE:
        return np.ones(k)
    levels = np.array([10, -10, 5, -5, 0])
    if k % 512:
        return np.exp2(np.random.permutation(np.resize(levels, k // 32))).repeat(32)
    a = np.empty((k // 512, 16))
    for p in range(k // 512):
        a[p, :8] = np.random.permutation(np.resize(levels, 8))
        for g in range(8):
            far = levels[np.abs(levels - a[p, g]) >= 10]
            a[p, g + 8] = far[np.random.randint(len(far))]
    return np.exp2(a.ravel()).repeat(32)


def f64(x):
    return np.asarray(x).astype(np.float64)


def striped(idx):
    return np.tile(idx.reshape(-1, 16).T, (8, 1)).astype(np.uint16)


def unstriped(offs):
    return offs[:16].T.reshape(-1).astype(np.int64)


def striped8(idx):
    return np.concatenate([x.reshape(-1, 16).T for x in idx]).astype(np.uint16)


def runs(offs, k):
    lists = np.stack([offs[16 * r : 16 * r + 16].T.reshape(-1) for r in range(8)]).astype(np.int64)
    return lists[np.arange(k) % 512 // 64]


def pack_weight(w):
    k, n = w.shape
    w = f64(np.asarray(w, np.float32).astype(ml_dtypes.bfloat16)).reshape(k // 32, 32, n)
    amax = np.abs(w).max(1)
    byte = np.clip(np.where(amax > 0, np.frexp(amax)[1] - 1 + 127 - 7, 1), 1, 254)
    scaled = (w * np.exp2(127.0 - byte)[:, None, :]).reshape(k, n).astype(np.float32)
    words = np.ascontiguousarray(scaled.reshape(k // 512, 128, 4, n).transpose(0, 1, 3, 2)).astype(ml_dtypes.float8_e4m3fn).view(np.uint8)
    return words, np.ascontiguousarray(byte.astype(np.uint8).reshape(k // 512, 16, n))


def unpack_weight(words, scales):
    g, p, n, _ = words.shape
    vals = np.ascontiguousarray(words).view(ml_dtypes.float8_e4m3fn).astype(np.float64) * np.repeat(np.exp2(scales.astype(np.float64) - 127.0), 8, axis=1)[..., None]
    return vals.transpose(0, 1, 3, 2).reshape(g * 512, n)


E2M1 = np.array([0.0, 0.5, 1.0, 1.5, 2.0, 3.0, 4.0, 6.0, -0.0, -0.5, -1.0, -1.5, -2.0, -3.0, -4.0, -6.0])


def pack_fp4(w):
    k, n = w.shape
    w = f64(np.asarray(w, np.float32).astype(ml_dtypes.bfloat16)).reshape(k // 32, 32, n)
    amax = np.abs(w).max(1)
    mant, ex = np.frexp(amax / 6.0)
    byte = np.clip(np.where(amax > 0, np.where(mant > 0.5, ex, ex - 1) + 127, 1), 1, 254)
    scaled = (w * np.exp2(127.0 - byte)[:, None, :]).reshape(k, n).astype(np.float32)
    c = np.ascontiguousarray(scaled.reshape(k // 512, 128, 4, n).transpose(0, 1, 3, 2)).astype(ml_dtypes.float4_e2m1fn).view(np.uint8) & 0xF
    words = (c[..., 0::2] | (c[..., 1::2] << 4)).reshape(k // 512, 128, 2 * n)
    return np.ascontiguousarray(words), np.ascontiguousarray(byte.astype(np.uint8).reshape(k // 512, 16, n))


def unpack_fp4(words, scales):
    g, _, n = scales.shape
    words = np.ascontiguousarray(words).reshape(g, 128, n, 2)
    nib = np.empty((g, 128, n, 4), np.uint8)
    nib[..., 0::2] = words & 0xF
    nib[..., 1::2] = words >> 4
    vals = E2M1[nib] * np.repeat(np.exp2(scales.astype(np.float64) - 127.0), 8, axis=1)[..., None]
    return vals.transpose(0, 1, 3, 2).reshape(g * 512, n)


def planes(y):
    n, m = y.shape
    v = y.astype(np.float32).astype(ml_dtypes.bfloat16).astype(np.float64).reshape(n // 32, 32, m)
    top = np.abs(v).max(1)
    byte = np.clip(np.where(top > 0, np.frexp(top)[1] - 1 + 127 - 7, 1), 1, 254)
    codes = (v * np.exp2(127.0 - byte)[:, None, :]).reshape(n, m).astype(np.float32).astype(ml_dtypes.float8_e4m3fn).view(np.uint8)
    words = codes.reshape(n // 512, 128, 4, m).transpose(0, 1, 3, 2)
    return np.ascontiguousarray(words), np.ascontiguousarray(byte.astype(np.uint8).reshape(n // 512, 16, m))


K, T, S, H = 512, 2048, 512, 512


def setup_inputs():
    n = np.random.standard_normal
    s = mx_kscale(K)[:, None]
    u = mx_kscale(S)
    packed_xT = pack_weight(n((K, T)) * s)
    packed_w1 = pack_fp4(n((K, H)) / np.sqrt(K) / s)
    return {
        "x_words": packed_xT[0],
        "x_scales": packed_xT[1],
        "w1_words": packed_w1[0],
        "w1_scales": packed_w1[1],
        "ga": (np.random.uniform(0.5, 1.5, (H, 1)) * u[:, None]).astype(np.float32),
        "gb": (np.random.uniform(0.5, 1.5, (H, 1)) / u[:, None]).astype(np.float32),
        "offs": striped(np.random.permutation(T)[:S]),
        "n1": striped8(np.stack([np.random.permutation(S) for _ in range(8)])),
        "n2": striped8(np.stack([np.random.permutation(S) for _ in range(8)])),
        "n3": striped8(np.stack([np.random.permutation(S) for _ in range(8)])),
        "n4": striped8(np.stack([np.random.permutation(S) for _ in range(8)])),
        "n5": striped8(np.stack([np.random.permutation(S) for _ in range(8)])),
        "n6": striped8(np.stack([np.random.permutation(S) for _ in range(8)])),
        "n7": striped8(np.stack([np.random.permutation(S) for _ in range(8)])),
    }


def reference(x_words, x_scales, w1_words, w1_scales, ga, gb, offs, n1, n2, n3, n4, n5, n6, n7):
    xq = unpack_weight(x_words, x_scales)[:, unstriped(offs)]
    y = unpack_fp4(w1_words, w1_scales).T @ xq
    z = f64(ga) * ((y[np.arange(H)[:, None], runs(n1, H)]) * (y[np.arange(H)[:, None], runs(n2, H)]))
    b1 = y[np.arange(H)[:, None], runs(n3, H)]
    b2 = y[np.arange(H)[:, None], runs(n4, H)]
    b3 = y[np.arange(H)[:, None], runs(n5, H)]
    z2 = f64(gb) * (np.maximum(np.maximum(b1, b2), b3) - (0.5 * (np.maximum(np.minimum(b1, b2), np.minimum(np.maximum(b1, b2), b3)))))
    s = 0.0625 * ((mxq(z, 0, "e4m3").T @ mxq(z2, 0, "e4m3")))
    pa = s[np.arange(S)[:, None], runs(n6, S)]
    pb = s[np.arange(S)[:, None], runs(n7, S)]
    out_0 = np.maximum(np.minimum(s, pa), np.minimum(np.maximum(s, pa), pb))
    return (out_0,) + planes(out_0)

@@ -1,0 +1,289 @@
+from contextlib import ExitStack
+
+import concourse.mybir as mybir
+from concourse.masks import make_identity
+
+K, T, S, H = 512, 2048, 512, 512
+FLOPS = 2 * K * H * S + 2 * H * S * S
+
+F32 = mybir.dt.float32
+BF16 = mybir.dt.bfloat16
+I32 = mybir.dt.int32
+U32 = mybir.dt.uint32
+U16 = mybir.dt.uint16
+U8 = mybir.dt.uint8
+FP8X4 = mybir.dt.float8_e4m3fn_x4
+FP4X4 = mybir.dt.float4_e2m1fn_x4
+ALU = mybir.AluOpType
+ACT = mybir.ActivationFunctionType
+
+P = 128
+PACK = 4
+WINDOW = 2 * S
+VECTOR_SHARE = 88
+
+
+def tile_picked_selfprodtop2med_none_po_kernel(
+    tc, x_words, x_scales, w1_words, w1_scales, ga, gb, offs, n1, n2, n3, n4, n5, n6, n7, out_0, out_1, out_2
+):
+    nc = tc.nc
+    with ExitStack() as ctx:
+        keep = ctx.enter_context(tc.tile_pool(name="keep", bufs=1))
+        psum = ctx.enter_context(tc.psum_pool(name="psum", bufs=1))
+
+        def sbuf(name, shape, dtype):
+            return keep.tile(shape, dtype, name=name, align_bytes=64)
+
+        def per_tile(name, width):
+            return [sbuf("%s%d" % (name, t), [P, width], F32) for t in range(PACK)]
+
+        lists = {}
+        for name in ("offs", "n1", "n2", "n3", "n4", "n5", "n6", "n7"):
+            lists[name] = sbuf(name, [P, S // 16], U16)
+
+        x_table = sbuf("x_table", [P, T], I32)
+        x_scale_table = sbuf("x_scale_table", [P, T], U8)
+        w_raw = sbuf("w_raw", [P, 2 * H], U8)
+        w_scale_raw = sbuf("w_scale_raw", [P, H], U8)
+        ga_sb = sbuf("ga_sb", [P, PACK], F32)
+        gb_sb = sbuf("gb_sb", [P, PACK], F32)
+
+        nc.vector.memset(x_scale_table[:].bitcast(I32), 0)
+        nc.gpsimd.memset(w_scale_raw[:].bitcast(I32), 0)
+
+        def load_scale_rows(queue, tile, src, q):
+            queue.dma_start(tile[32 * q : 32 * q + 4, :].bitcast(I32), src[0, 4 * q : 4 * q + 4, :].bitcast(I32))
+
+        nc.sync.dma_start(lists["offs"][:], offs)
+        nc.sync.dma_start(w_raw[:].bitcast(I32), w1_words[0].bitcast(I32))
+        nc.sync.dma_start(x_table[:], x_words[0].rearrange("p n t -> p (n t)").bitcast(I32))
+        for q in range(4):
+            load_scale_rows(nc.sync, x_scale_table, x_scales, q)
+        nc.sync.dma_start(gb_sb[:], gb.rearrange("(p t) o -> p (t o)", t=PACK))
+        for q in range(4):
+            load_scale_rows(nc.sync if q < 2 else nc.gpsimd, w_scale_raw, w1_scales, q)
+        for name, src in (("n3", n3), ("n4", n4), ("n5", n5)):
+            nc.sync.dma_start(lists[name][:], src)
+        nc.sync.dma_start(ga_sb[:], ga.rearrange("(p t) o -> p (t o)", t=PACK))
+        for name, src in (("n1", n1), ("n2", n2), ("n6", n6), ("n7", n7)):
+            nc.sync.dma_start(lists[name][:], src)
+
+        ident = sbuf("ident", [P, P], F32)
+        make_identity(nc, ident[:])
+
+        half_gb = sbuf("half_gb", [P, PACK], F32)
+        nc.scalar.activation(half_gb[:], gb_sb[:], ACT.Abs, scale=0.5)
+        gb_sign = sbuf("gb_sign", [P, PACK], F32)
+        gb_step = sbuf("gb_step", [P, PACK], F32)
+        ga_signed = sbuf("ga_signed", [P, PACK], F32)
+        nc.gpsimd.tensor_scalar(gb_step[:], gb_sb[:], 0.0, 2.0, ALU.is_ge, ALU.mult)
+        nc.gpsimd.tensor_scalar(gb_sign[:], gb_step[:], 1.0, -1.0, ALU.mult, ALU.add)
+        nc.gpsimd.tensor_tensor(ga_signed[:], gb_sign[:], ga_sb[:], ALU.mult)
+
+        w_dealt = sbuf("w_dealt", [P, 2 * H], U8)
+        w_scale_dealt = sbuf("w_scale_dealt", [P, H], U8)
+        x_picked = sbuf("x_picked", [P, S], I32)
+        x_scale_picked = sbuf("x_scale_picked", [P, S], U8)
+        nc.vector.tensor_copy(
+            w_dealt[:].rearrange("p (t m b) -> p m t b", t=PACK, b=2),
+            w_raw[:].rearrange("p (m t b) -> p m t b", t=PACK, b=2),
+        )
+        nc.vector.tensor_copy(x_scale_picked[:], x_scale_table[:].indirect(lists["offs"][:]))
+        nc.vector.tensor_copy(
+            w_scale_dealt[:].rearrange("p (t m) -> p m t", t=PACK),
+            w_scale_raw[:].rearrange("p (m t) -> p m t", t=PACK),
+        )
+        halves = (slice(0, S // 2), slice(S // 2, S))
+
+        def entries(name, cols):
+            return lists[name][:, cols.start // 16 : cols.stop // 16]
+
+        for cols in halves:
+            nc.vector.tensor_copy(
+                x_picked[:, cols].bitcast(U32), x_table[:].bitcast(U32).indirect(entries("offs", cols))
+            )
+
+        banks_a = [psum.tile([P, S], F32, name="bank_a%d" % t) for t in range(PACK)]
+        banks_b = [psum.tile([P, S], F32, name="bank_b%d" % t) for t in range(PACK)]
+
+        def pieces(banks, spare, t):
+            if t == 0:
+                return [(halves[0], banks[0][:, halves[0]]), (halves[1], spare[:, halves[1]])]
+            return [(slice(0, S), banks[t][:])]
+
+        for t in range(PACK):
+            for cols, bank in pieces(banks_a, banks_b[0], t):
+                nc.tensor.matmul_mx(
+                    out=bank,
+                    lhsT=w_dealt[:, 2 * P * t : 2 * P * (t + 1)].bitcast(FP4X4),
+                    lhsT_scale=w_scale_dealt[:, P * t : P * (t + 1)],
+                    rhs=x_picked[:, cols].bitcast(FP8X4),
+                    rhs_scale=x_scale_picked[:, cols],
+                    start=True,
+                    stop=True,
+                )
+
+        yb = per_tile("yb", WINDOW)
+        ya = per_tile("ya", WINDOW)
+        y = per_tile("y", WINDOW)
+        first = per_tile("first", S)
+        diff = per_tile("diff", S)
+        absdiff = per_tile("absdiff", S)
+        edge = per_tile("edge", S)
+        over = per_tile("over", S)
+        clip = per_tile("clip", S)
+        rise = per_tile("rise", S)
+        turned = per_tile("turned", S)
+
+        def gathered(window, name):
+            return window[:].indirect(lists[name][:])
+
+        for t in range(PACK):
+            for cols, bank in pieces(banks_a, banks_b[0], t):
+                nc.scalar.activation(yb[t][:, cols], bank, ACT.Copy, scale=half_gb[:, t : t + 1])
+
+        def top_sum(t):
+            for jb in range(4):
+                cols = slice(P * jb, P * (jb + 1))
+                for i, term in enumerate((edge, rise, clip)):
+                    nc.tensor.matmul(
+                        banks_b[t][:, cols], term[t][:, cols], ident[:], start=(i == 0), stop=(i == 2), is_transpose=True
+                    )
+            nc.scalar.copy(turned[t][:], banks_b[t][:])
+            for jb in range(4):
+                nc.tensor.transpose(banks_a[jb][:, P * t : P * (t + 1)], turned[t][:, P * jb : P * (jb + 1)], ident[:])
+
+        for pair in ((0, 1), (2, 3)):
+            for t in pair:
+                nc.vector.tensor_copy(first[t][:], gathered(yb[t], "n3"))
+            for t in pair:
+                nc.vector.tensor_tensor(diff[t][:], gathered(yb[t], "n4"), first[t][:], ALU.subtract)
+                nc.scalar.activation(absdiff[t][:], diff[t][:], ACT.Abs)
+            for t in pair:
+                nc.vector.scalar_tensor_tensor(edge[t][:], diff[t][:], 0.0, first[t][:], ALU.max, ALU.add)
+            if pair[0] == 0:
+                for t in range(PACK):
+                    for cols, bank in pieces(banks_a, banks_b[0], t):
+                        nc.scalar.copy(y[t][:, cols], bank)
+                        nc.scalar.activation(ya[t][:, cols], bank, ACT.Copy, scale=ga_signed[:, t : t + 1])
+            for t in pair:
+                nc.vector.tensor_tensor(over[t][:], gathered(yb[t], "n5"), edge[t][:], ALU.subtract)
+                nc.scalar.activation(rise[t][:], over[t][:], ACT.Relu, scale=3.0)
+            for t in pair:
+                nc.vector.scalar_tensor_tensor(clip[t][:], over[t][:], -1.0, absdiff[t][:], ALU.mult, ALU.min)
+            for t in pair:
+                top_sum(t)
+
+        z2_bf = sbuf("z2_bf", [P, S * PACK], BF16)
+        z2_codes = sbuf("z2_codes", [P, S], U32)
+        z2_scales = sbuf("z2_scales", [P, S], U8)
+        for jb in range(4):
+            nc.scalar.copy(
+                z2_bf[:, PACK * P * jb : PACK * P * (jb + 1)].rearrange("p (j t) -> p j t", t=PACK),
+                banks_a[jb][:].rearrange("p (t j) -> p j t", t=PACK),
+            )
+
+        z = sbuf("z", [P, PACK, S], F32)
+        z_bf = sbuf("z_bf", [P, S * PACK], BF16)
+        z_codes = sbuf("z_codes", [P, S], U32)
+        z_scales = sbuf("z_scales", [P, S], U8)
+        z_dst = z_bf[:].rearrange("p (u m t) -> p m u t", u=PACK, t=PACK)
+        z_src = z[:].rearrange("p t (m u) -> p m u t", u=PACK)
+        for pair in ((2, 3), (0, 1)):
+            for t in pair:
+                nc.vector.tensor_copy(over[2 + t % 2][:], gathered(ya[t], "n1"))
+            if pair[0] == 0:
+                nc.vector.quantize_mx(out=z2_codes[:].bitcast(FP8X4), scales=z2_scales[:], in_=z2_bf[:])
+            for t in pair:
+                nc.vector.tensor_tensor(z[:, t, :], gathered(y[t], "n2"), over[2 + t % 2][:], ALU.mult)
+            if pair[0] == 2:
+                nc.scalar.copy(z_dst[:, :, :, 2:4], z_src[:, :, :, 2:4])
+        nc.vector.tensor_copy(z_dst[:, 0:VECTOR_SHARE, :, 0:2], z_src[:, 0:VECTOR_SHARE, :, 0:2])
+        nc.scalar.copy(z_dst[:, VECTOR_SHARE:P, :, 0:2], z_src[:, VECTOR_SHARE:P, :, 0:2])
+        for u in range(PACK):
+            rows = slice(P * u, P * (u + 1))
+            nc.vector.quantize_mx(
+                out=z_codes[:, rows].bitcast(FP8X4), scales=z_scales[:, rows], in_=z_bf[:, S * u : S * (u + 1)]
+            )
+            for cols, bank in pieces(banks_b, banks_a[0], u):
+                nc.tensor.matmul_mx(
+                    out=bank,
+                    lhsT=z_codes[:, rows].bitcast(FP8X4),
+                    lhsT_scale=z_scales[:, rows],
+                    rhs=z2_codes[:, cols].bitcast(FP8X4),
+                    rhs_scale=z2_scales[:, cols],
+                    start=True,
+                    stop=True,
+                )
+
+        s_window = yb
+        s_plain = first
+        result = sbuf("result", [P, PACK, S], F32)
+        out_rows = out_0.rearrange("(p t) j -> p t j", t=PACK)
+        (cols_a, bank_lo), (cols_b, bank_hi) = pieces(banks_b, banks_a[0], 0)
+        nc.scalar.activation(s_window[0][:, cols_a], bank_lo, ACT.Copy, scale=0.0625)
+        nc.vector.tensor_scalar(s_window[0][:, cols_b], bank_hi, 0.0625, None, ALU.mult)
+        nc.scalar.activation(s_plain[0][:, cols_b], bank_hi, ACT.Copy, scale=0.0625)
+        nc.vector.tensor_scalar(s_plain[0][:, cols_a], bank_lo, 0.0625, None, ALU.mult)
+        for t in range(1, PACK):
+            nc.scalar.activation(s_window[t][:, 0:S], banks_b[t][:], ACT.Copy, scale=0.0625)
+            nc.scalar.activation(s_plain[t][:], banks_b[t][:], ACT.Copy, scale=0.0625)
+
+        out_bf = sbuf("out_bf", [P, S * PACK], BF16)
+        out_codes = sbuf("out_codes", [P, S], I32)
+        out_scales = sbuf("out_scales", [P, S], U8)
+        o_dst = out_bf[:].rearrange("p (j t) -> p j t", t=PACK)
+        o_src = result[:].rearrange("p t j -> p j t")
+
+        def median_sum(t):
+            for jb in range(4):
+                cols = slice(P * jb, P * (jb + 1))
+                for i, term in enumerate((edge, clip)):
+                    nc.tensor.matmul(
+                        banks_a[t][:, cols], term[t][:, cols], ident[:], start=(i == 0), stop=(i == 1), is_transpose=True
+                    )
+            nc.scalar.copy(turned[t][:], banks_a[t][:])
+            for jb in range(4):
+                cols = slice(P * jb, P * (jb + 1))
+                nc.tensor.transpose(banks_a[2 + t][:, cols], turned[t][:, cols], ident[:])
+            nc.scalar.copy(result[:, t, :], banks_a[2 + t][:])
+            nc.sync.dma_start(out_rows[:, t, :], result[:, t, :])
+
+        for pair in ((0, 1), (2, 3)):
+            for t in pair:
+                nc.vector.tensor_tensor(diff[t][:], gathered(s_window[t], "n6"), s_plain[t][:], ALU.subtract)
+                nc.scalar.activation(absdiff[t][:], diff[t][:], ACT.Abs)
+            if pair[0] == 2:
+                median_sum(0)
+                median_sum(1)
+                nc.scalar.copy(o_dst[:, :, 0:2], o_src[:, :, 0:2])
+            for t in pair:
+                nc.vector.scalar_tensor_tensor(edge[t][:], diff[t][:], 0.0, s_plain[t][:], ALU.min, ALU.add)
+            for t in pair:
+                nc.vector.tensor_tensor(over[t][:], gathered(s_window[t], "n7"), edge[t][:], ALU.subtract)
+            if pair[0] == 0:
+                for t in pair:
+                    nc.vector.scalar_tensor_tensor(clip[t][:], over[t][:], 0.0, absdiff[t][:], ALU.max, ALU.min)
+
+        nc.vector.scalar_tensor_tensor(clip[2][:], over[2][:], 0.0, absdiff[2][:], ALU.max, ALU.min)
+        for cols in halves:
+            nc.vector.scalar_tensor_tensor(clip[3][:, cols], over[3][:, cols], 0.0, absdiff[3][:, cols], ALU.max, ALU.min)
+        nc.vector.tensor_tensor(result[:, 2, :], edge[2][:], clip[2][:], ALU.add)
+        nc.sync.dma_start(out_rows[:, 2, :], result[:, 2, :])
+        for cols in halves:
+            nc.vector.tensor_tensor(result[:, 3, cols], edge[3][:, cols], clip[3][:, cols], ALU.add)
+        nc.sync.dma_start(out_rows[:, 3, :], result[:, 3, :])
+        nc.scalar.copy(o_dst[:, halves[0], 2:4], o_src[:, halves[0], 2:4])
+        nc.vector.tensor_copy(o_dst[:, halves[1], 2:4], o_src[:, halves[1], 2:4])
+        words_out = out_1[0].rearrange("p n t -> p (n t)").bitcast(I32)
+        for cols in (halves[1], halves[0]):
+            nc.vector.quantize_mx(
+                out=out_codes[:, cols].bitcast(FP8X4),
+                scales=out_scales[:, cols],
+                in_=out_bf[:, PACK * cols.start : PACK * cols.stop],
+            )
+        nc.sync.dma_start(words_out, out_codes[:])
+        for q in range(4):
+            nc.scalar.dma_start(
+                out_2[0, 4 * q : 4 * q + 4, :].bitcast(I32), out_scales[32 * q : 32 * q + 4, :].bitcast(I32)
+            )

@@ -21,6 +21,7 @@ P = 128
 PACK = 4
 WINDOW = 2 * S
 VECTOR_SHARE = 88
+CLEAR_SPLIT = 768
 
 
 def tile_picked_selfprodtop2med_none_po_kernel(
@@ -48,20 +49,23 @@ def tile_picked_selfprodtop2med_none_po_kernel(
         ga_sb = sbuf("ga_sb", [P, PACK], F32)
         gb_sb = sbuf("gb_sb", [P, PACK], F32)
 
-        nc.vector.memset(x_scale_table[:].bitcast(I32), 0)
-        nc.gpsimd.memset(w_scale_raw[:].bitcast(I32), 0)
+        nc.vector.memset(w_scale_raw[:].bitcast(I32), 0)
+        nc.vector.memset(x_scale_table[:, 0:CLEAR_SPLIT].bitcast(I32), 0)
+        nc.gpsimd.memset(x_scale_table[:, CLEAR_SPLIT:T].bitcast(I32), 0)
 
         def load_scale_rows(queue, tile, src, q):
             queue.dma_start(tile[32 * q : 32 * q + 4, :].bitcast(I32), src[0, 4 * q : 4 * q + 4, :].bitcast(I32))
 
         nc.sync.dma_start(lists["offs"][:], offs)
         nc.sync.dma_start(w_raw[:].bitcast(I32), w1_words[0].bitcast(I32))
-        nc.sync.dma_start(x_table[:], x_words[0].rearrange("p n t -> p (n t)").bitcast(I32))
+        x_rows = x_words[0].rearrange("p n t -> p (n t)").bitcast(I32)
+        nc.sync.dma_start(x_table[:, 0 : T // 2], x_rows[:, 0 : T // 2])
         for q in range(4):
             load_scale_rows(nc.sync, x_scale_table, x_scales, q)
-        nc.sync.dma_start(gb_sb[:], gb.rearrange("(p t) o -> p (t o)", t=PACK))
+        nc.sync.dma_start(x_table[:, T // 2 : T], x_rows[:, T // 2 : T])
         for q in range(4):
             load_scale_rows(nc.sync if q < 2 else nc.gpsimd, w_scale_raw, w1_scales, q)
+        nc.sync.dma_start(gb_sb[:], gb.rearrange("(p t) o -> p (t o)", t=PACK))
         for name, src in (("n3", n3), ("n4", n4), ("n5", n5)):
             nc.sync.dma_start(lists[name][:], src)
         nc.sync.dma_start(ga_sb[:], ga.rearrange("(p t) o -> p (t o)", t=PACK))
@@ -89,123 +93,155 @@ def tile_picked_selfprodtop2med_none_po_kernel(
             w_raw[:].rearrange("p (m t b) -> p m t b", t=PACK, b=2),
         )
         nc.vector.tensor_copy(x_scale_picked[:], x_scale_table[:].indirect(lists["offs"][:]))
-        nc.vector.tensor_copy(
-            w_scale_dealt[:].rearrange("p (t m) -> p m t", t=PACK),
-            w_scale_raw[:].rearrange("p (m t) -> p m t", t=PACK),
-        )
         halves = (slice(0, S // 2), slice(S // 2, S))
 
         def entries(name, cols):
             return lists[name][:, cols.start // 16 : cols.stop // 16]
 
-        for cols in halves:
+        scale_dst = w_scale_dealt[:].rearrange("p (t m) -> p m t", t=PACK)
+        scale_src = w_scale_raw[:].rearrange("p (m t) -> p m t", t=PACK)
+        for cols, planes in zip(halves, (slice(0, 2), slice(2, PACK))):
             nc.vector.tensor_copy(
                 x_picked[:, cols].bitcast(U32), x_table[:].bitcast(U32).indirect(entries("offs", cols))
             )
+            nc.vector.tensor_copy(scale_dst[:, :, planes], scale_src[:, :, planes])
 
         banks_a = [psum.tile([P, S], F32, name="bank_a%d" % t) for t in range(PACK)]
         banks_b = [psum.tile([P, S], F32, name="bank_b%d" % t) for t in range(PACK)]
 
-        def pieces(banks, spare, t):
-            if t == 0:
-                return [(halves[0], banks[0][:, halves[0]]), (halves[1], spare[:, halves[1]])]
-            return [(slice(0, S), banks[t][:])]
+        def first_product(t, cols, bank):
+            nc.tensor.matmul_mx(
+                out=bank,
+                lhsT=w_dealt[:, 2 * P * t : 2 * P * (t + 1)].bitcast(FP4X4),
+                lhsT_scale=w_scale_dealt[:, P * t : P * (t + 1)],
+                rhs=x_picked[:, cols].bitcast(FP8X4),
+                rhs_scale=x_scale_picked[:, cols],
+                start=True,
+                stop=True,
+            )
 
-        for t in range(PACK):
-            for cols, bank in pieces(banks_a, banks_b[0], t):
-                nc.tensor.matmul_mx(
-                    out=bank,
-                    lhsT=w_dealt[:, 2 * P * t : 2 * P * (t + 1)].bitcast(FP4X4),
-                    lhsT_scale=w_scale_dealt[:, P * t : P * (t + 1)],
-                    rhs=x_picked[:, cols].bitcast(FP8X4),
-                    rhs_scale=x_scale_picked[:, cols],
-                    start=True,
-                    stop=True,
-                )
+        y_parts = [[(halves[0], banks_a[t][:, halves[0]]), (halves[1], banks_b[t][:, halves[1]])] for t in (0, 1)]
+        y_parts = y_parts + [[(slice(0, S), banks_a[t][:])] for t in (2, 3)]
+        for h in (0, 1):
+            for t in (0, 1):
+                first_product(t, *y_parts[t][h])
+        for t in (2, 3):
+            first_product(t, *y_parts[t][0])
 
         yb = per_tile("yb", WINDOW)
         ya = per_tile("ya", WINDOW)
         y = per_tile("y", WINDOW)
-        first = per_tile("first", S)
-        diff = per_tile("diff", S)
+        z = sbuf("z", [P, PACK, S], F32)
+        work = [sbuf("work%d" % i, [P, S], F32) for i in range(8)]
+        first = [work[0][:], work[1][:], work[2][:], z[:, 2, :]]
+        lift = [work[3][:], work[4][:], work[5][:], z[:, 3, :]]
+        diff = [work[6][:], work[7][:], first[1], lift[1]]
         absdiff = per_tile("absdiff", S)
         edge = per_tile("edge", S)
         over = per_tile("over", S)
         clip = per_tile("clip", S)
         rise = per_tile("rise", S)
-        turned = per_tile("turned", S)
 
         def gathered(window, name):
             return window[:].indirect(lists[name][:])
 
-        for t in range(PACK):
-            for cols, bank in pieces(banks_a, banks_b[0], t):
-                nc.scalar.activation(yb[t][:, cols], bank, ACT.Copy, scale=half_gb[:, t : t + 1])
+        for t, h in ((0, 0), (1, 0), (1, 1), (2, 0), (3, 0)):
+            cols, bank = y_parts[t][h]
+            nc.scalar.activation(yb[t][:, cols], bank, ACT.Copy, scale=half_gb[:, t : t + 1])
+        cols, bank = y_parts[0][1]
+        nc.vector.tensor_scalar(yb[0][:, cols], bank, half_gb[:, 0:1], None, ALU.mult)
 
-        def top_sum(t):
-            for jb in range(4):
-                cols = slice(P * jb, P * (jb + 1))
-                for i, term in enumerate((edge, rise, clip)):
-                    nc.tensor.matmul(
-                        banks_b[t][:, cols], term[t][:, cols], ident[:], start=(i == 0), stop=(i == 2), is_transpose=True
-                    )
-            nc.scalar.copy(turned[t][:], banks_b[t][:])
-            for jb in range(4):
-                nc.tensor.transpose(banks_a[jb][:, P * t : P * (t + 1)], turned[t][:, P * jb : P * (jb + 1)], ident[:])
+        def plain_windows(t):
+            for cols, bank in y_parts[t]:
+                nc.scalar.activation(ya[t][:, cols], bank, ACT.Copy, scale=ga_signed[:, t : t + 1])
+                nc.scalar.copy(y[t][:, cols], bank)
 
-        for pair in ((0, 1), (2, 3)):
+        def differences(pair):
             for t in pair:
-                nc.vector.tensor_copy(first[t][:], gathered(yb[t], "n3"))
-            for t in pair:
-                nc.vector.tensor_tensor(diff[t][:], gathered(yb[t], "n4"), first[t][:], ALU.subtract)
-                nc.scalar.activation(absdiff[t][:], diff[t][:], ACT.Abs)
-            for t in pair:
-                nc.vector.scalar_tensor_tensor(edge[t][:], diff[t][:], 0.0, first[t][:], ALU.max, ALU.add)
-            if pair[0] == 0:
-                for t in range(PACK):
-                    for cols, bank in pieces(banks_a, banks_b[0], t):
-                        nc.scalar.copy(y[t][:, cols], bank)
-                        nc.scalar.activation(ya[t][:, cols], bank, ACT.Copy, scale=ga_signed[:, t : t + 1])
+                nc.vector.tensor_tensor(diff[t], gathered(yb[t], "n4"), first[t], ALU.subtract)
+                nc.scalar.activation(lift[t], diff[t], ACT.Relu)
+                nc.scalar.activation(absdiff[t][:], diff[t], ACT.Abs)
+                nc.gpsimd.tensor_tensor(edge[t][:], first[t], lift[t], ALU.add)
+
+        def third(pair):
             for t in pair:
                 nc.vector.tensor_tensor(over[t][:], gathered(yb[t], "n5"), edge[t][:], ALU.subtract)
                 nc.scalar.activation(rise[t][:], over[t][:], ACT.Relu, scale=3.0)
             for t in pair:
                 nc.vector.scalar_tensor_tensor(clip[t][:], over[t][:], -1.0, absdiff[t][:], ALU.mult, ALU.min)
             for t in pair:
-                top_sum(t)
+                for jb in range(4):
+                    cols = slice(P * jb, P * (jb + 1))
+                    for i, term in enumerate((edge, rise, clip)):
+                        nc.tensor.matmul(
+                            banks_b[jb][:, P * t : P * (t + 1)],
+                            term[t][:, cols],
+                            ident[:],
+                            start=(i == 0),
+                            stop=(i == 2),
+                            is_transpose=True,
+                        )
 
+        plain_windows(2)
+        plain_windows(3)
+        for t in (0, 1):
+            nc.vector.tensor_copy(first[t], gathered(yb[t], "n3"))
+        differences((0, 1))
+        for t in (2, 3):
+            nc.vector.tensor_copy(first[t], gathered(yb[t], "n3"))
+        plain_windows(0)
+        plain_windows(1)
+        third((0, 1))
+        differences((2, 3))
+        factor = [absdiff[1][:], over[1][:]]
+        for t in (2, 3):
+            nc.vector.tensor_copy(factor[t % 2], gathered(ya[t], "n1"))
+        third((2, 3))
+
+        z2_turned = sbuf("z2_turned", [P, 4, S], BF16)
         z2_bf = sbuf("z2_bf", [P, S * PACK], BF16)
         z2_codes = sbuf("z2_codes", [P, S], U32)
         z2_scales = sbuf("z2_scales", [P, S], U8)
         for jb in range(4):
             nc.scalar.copy(
-                z2_bf[:, PACK * P * jb : PACK * P * (jb + 1)].rearrange("p (j t) -> p j t", t=PACK),
-                banks_a[jb][:].rearrange("p (t j) -> p j t", t=PACK),
+                z2_turned[:, jb, :].rearrange("j (u p e) -> j u p e", u=2, e=2),
+                banks_b[jb][:].rearrange("j (u e p) -> j u p e", u=2, e=2),
             )
+            pairs = z2_turned[:, jb, :].bitcast(F32)
+            for u in (0, 1):
+                slot = 2 * (jb % 2) + u
+                nc.tensor.transpose(
+                    banks_a[jb // 2][:, P * slot : P * (slot + 1)], pairs[:, P * u : P * (u + 1)], ident[:]
+                )
+            if jb % 2 == 1:
+                nc.scalar.copy(
+                    z2_bf[:, 2 * S * (jb // 2) : 2 * S * (jb // 2 + 1)].bitcast(F32).rearrange("p (b j u) -> p b j u", b=2, u=2),
+                    banks_a[jb // 2][:].rearrange("p (b u j) -> p b j u", b=2, u=2),
+                )
 
-        z = sbuf("z", [P, PACK, S], F32)
         z_bf = sbuf("z_bf", [P, S * PACK], BF16)
         z_codes = sbuf("z_codes", [P, S], U32)
         z_scales = sbuf("z_scales", [P, S], U8)
         z_dst = z_bf[:].rearrange("p (u m t) -> p m u t", u=PACK, t=PACK)
         z_src = z[:].rearrange("p t (m u) -> p m u t", u=PACK)
-        for pair in ((2, 3), (0, 1)):
-            for t in pair:
-                nc.vector.tensor_copy(over[2 + t % 2][:], gathered(ya[t], "n1"))
-            if pair[0] == 0:
-                nc.vector.quantize_mx(out=z2_codes[:].bitcast(FP8X4), scales=z2_scales[:], in_=z2_bf[:])
-            for t in pair:
-                nc.vector.tensor_tensor(z[:, t, :], gathered(y[t], "n2"), over[2 + t % 2][:], ALU.mult)
-            if pair[0] == 2:
-                nc.scalar.copy(z_dst[:, :, :, 2:4], z_src[:, :, :, 2:4])
+        for t in (2, 3):
+            nc.vector.tensor_tensor(z[:, t, :], gathered(y[t], "n2"), factor[t % 2], ALU.mult)
+        nc.scalar.copy(z_dst[:, :, :, 2:4], z_src[:, :, :, 2:4])
+        for t in (0, 1):
+            nc.vector.tensor_copy(factor[t], gathered(ya[t], "n1"))
+        nc.vector.quantize_mx(out=z2_codes[:].bitcast(FP8X4), scales=z2_scales[:], in_=z2_bf[:])
+        for t in (0, 1):
+            nc.vector.tensor_tensor(z[:, t, :], gathered(y[t], "n2"), factor[t], ALU.mult)
         nc.vector.tensor_copy(z_dst[:, 0:VECTOR_SHARE, :, 0:2], z_src[:, 0:VECTOR_SHARE, :, 0:2])
         nc.scalar.copy(z_dst[:, VECTOR_SHARE:P, :, 0:2], z_src[:, VECTOR_SHARE:P, :, 0:2])
+        s_parts = [[(halves[0], banks_b[0][:, halves[0]]), (halves[1], banks_a[2][:, halves[1]])]]
+        s_parts = s_parts + [[(slice(0, S), banks_b[t][:])] for t in (1, 2, 3)]
         for u in range(PACK):
             rows = slice(P * u, P * (u + 1))
             nc.vector.quantize_mx(
                 out=z_codes[:, rows].bitcast(FP8X4), scales=z_scales[:, rows], in_=z_bf[:, S * u : S * (u + 1)]
             )
-            for cols, bank in pieces(banks_b, banks_a[0], u):
+            for cols, bank in s_parts[u]:
                 nc.tensor.matmul_mx(
                     out=bank,
                     lhsT=z_codes[:, rows].bitcast(FP8X4),
@@ -217,10 +253,12 @@ def tile_picked_selfprodtop2med_none_po_kernel(
                 )
 
         s_window = yb
-        s_plain = first
+        s_plain = work[0:4]
+        diff = work[4:8]
+        turned = rise
         result = sbuf("result", [P, PACK, S], F32)
         out_rows = out_0.rearrange("(p t) j -> p t j", t=PACK)
-        (cols_a, bank_lo), (cols_b, bank_hi) = pieces(banks_b, banks_a[0], 0)
+        (cols_a, bank_lo), (cols_b, bank_hi) = s_parts[0]
         nc.scalar.activation(s_window[0][:, cols_a], bank_lo, ACT.Copy, scale=0.0625)
         nc.vector.tensor_scalar(s_window[0][:, cols_b], bank_hi, 0.0625, None, ALU.mult)
         nc.scalar.activation(s_plain[0][:, cols_b], bank_hi, ACT.Copy, scale=0.0625)

@@ -46,12 +46,12 @@ def tile_picked_selfprodtop2med_none_po_kernel(
         x_scale_table = sbuf("x_scale_table", [P, T], U8)
         w_raw = sbuf("w_raw", [P, 2 * H], U8)
         w_scale_raw = sbuf("w_scale_raw", [P, H], U8)
-        ga_sb = sbuf("ga_sb", [P, PACK], F32)
-        gb_sb = sbuf("gb_sb", [P, PACK], F32)
+        gain_rows = sbuf("gain_rows", [P, P], F32)
 
         nc.vector.memset(w_scale_raw[:].bitcast(I32), 0)
         nc.vector.memset(x_scale_table[:, 0:CLEAR_SPLIT].bitcast(I32), 0)
         nc.gpsimd.memset(x_scale_table[:, CLEAR_SPLIT:T].bitcast(I32), 0)
+        nc.vector.memset(gain_rows[:], 0.0)
 
         def load_scale_rows(queue, tile, src, q):
             queue.dma_start(tile[32 * q : 32 * q + 4, :].bitcast(I32), src[0, 4 * q : 4 * q + 4, :].bitcast(I32))
@@ -59,38 +59,31 @@ def tile_picked_selfprodtop2med_none_po_kernel(
         nc.sync.dma_start(lists["offs"][:], offs)
         nc.sync.dma_start(w_raw[:].bitcast(I32), w1_words[0].bitcast(I32))
         x_rows = x_words[0].rearrange("p n t -> p (n t)").bitcast(I32)
-        nc.sync.dma_start(x_table[:, 0 : T // 2], x_rows[:, 0 : T // 2])
+        nc.sync.dma_start(x_table[:, 0 : T // 4], x_rows[:, 0 : T // 4])
         for q in range(4):
             load_scale_rows(nc.sync, x_scale_table, x_scales, q)
-        nc.sync.dma_start(x_table[:, T // 2 : T], x_rows[:, T // 2 : T])
+        nc.sync.dma_start(x_table[:, T // 4 : T], x_rows[:, T // 4 : T])
         for q in range(4):
-            load_scale_rows(nc.sync if q < 2 else nc.gpsimd, w_scale_raw, w1_scales, q)
-        nc.sync.dma_start(gb_sb[:], gb.rearrange("(p t) o -> p (t o)", t=PACK))
-        for name, src in (("n3", n3), ("n4", n4), ("n5", n5)):
-            nc.sync.dma_start(lists[name][:], src)
-        nc.sync.dma_start(ga_sb[:], ga.rearrange("(p t) o -> p (t o)", t=PACK))
-        for name, src in (("n1", n1), ("n2", n2), ("n6", n6), ("n7", n7)):
+            load_scale_rows(nc.sync, w_scale_raw, w1_scales, q)
+        nc.sync.dma_start(lists["n3"][:], n3)
+        for first_row, gain in ((0, ga), (PACK, gb)):
+            nc.sync.dma_start(
+                gain_rows[first_row : first_row + PACK, :].rearrange("t (b c) -> t b c", c=8),
+                gain.rearrange("(b t c) o -> t b (c o)", t=PACK, c=8),
+            )
+        for name, src in (("n4", n4), ("n5", n5), ("n1", n1), ("n2", n2), ("n6", n6), ("n7", n7)):
             nc.sync.dma_start(lists[name][:], src)
 
         ident = sbuf("ident", [P, P], F32)
         make_identity(nc, ident[:])
-
-        half_gb = sbuf("half_gb", [P, PACK], F32)
-        nc.scalar.activation(half_gb[:], gb_sb[:], ACT.Abs, scale=0.5)
-        gb_sign = sbuf("gb_sign", [P, PACK], F32)
-        gb_step = sbuf("gb_step", [P, PACK], F32)
-        ga_signed = sbuf("ga_signed", [P, PACK], F32)
-        nc.gpsimd.tensor_scalar(gb_step[:], gb_sb[:], 0.0, 2.0, ALU.is_ge, ALU.mult)
-        nc.gpsimd.tensor_scalar(gb_sign[:], gb_step[:], 1.0, -1.0, ALU.mult, ALU.add)
-        nc.gpsimd.tensor_tensor(ga_signed[:], gb_sign[:], ga_sb[:], ALU.mult)
 
         w_dealt = sbuf("w_dealt", [P, 2 * H], U8)
         w_scale_dealt = sbuf("w_scale_dealt", [P, H], U8)
         x_picked = sbuf("x_picked", [P, S], I32)
         x_scale_picked = sbuf("x_scale_picked", [P, S], U8)
         nc.vector.tensor_copy(
-            w_dealt[:].rearrange("p (t m b) -> p m t b", t=PACK, b=2),
-            w_raw[:].rearrange("p (m t b) -> p m t b", t=PACK, b=2),
+            w_dealt[:].bitcast(I32).rearrange("p (t b c) -> p b t c", t=PACK, c=4),
+            w_raw[:].bitcast(I32).rearrange("p (b t c) -> p b t c", t=PACK, c=4),
         )
         nc.vector.tensor_copy(x_scale_picked[:], x_scale_table[:].indirect(lists["offs"][:]))
         halves = (slice(0, S // 2), slice(S // 2, S))
@@ -98,13 +91,14 @@ def tile_picked_selfprodtop2med_none_po_kernel(
         def entries(name, cols):
             return lists[name][:, cols.start // 16 : cols.stop // 16]
 
-        scale_dst = w_scale_dealt[:].rearrange("p (t m) -> p m t", t=PACK)
-        scale_src = w_scale_raw[:].rearrange("p (m t) -> p m t", t=PACK)
-        for cols, planes in zip(halves, (slice(0, 2), slice(2, PACK))):
+        nc.gpsimd.tensor_copy(
+            w_scale_dealt[:].bitcast(I32).rearrange("p (t b c) -> p b t c", t=PACK, c=2),
+            w_scale_raw[:].bitcast(I32).rearrange("p (b t c) -> p b t c", t=PACK, c=2),
+        )
+        for cols in halves:
             nc.vector.tensor_copy(
                 x_picked[:, cols].bitcast(U32), x_table[:].bitcast(U32).indirect(entries("offs", cols))
             )
-            nc.vector.tensor_copy(scale_dst[:, :, planes], scale_src[:, :, planes])
 
         banks_a = [psum.tile([P, S], F32, name="bank_a%d" % t) for t in range(PACK)]
         banks_b = [psum.tile([P, S], F32, name="bank_b%d" % t) for t in range(PACK)]
@@ -128,51 +122,73 @@ def tile_picked_selfprodtop2med_none_po_kernel(
         for t in (2, 3):
             first_product(t, *y_parts[t][0])
 
-        yb = per_tile("yb", WINDOW)
         ya = per_tile("ya", WINDOW)
         y = per_tile("y", WINDOW)
-        z = sbuf("z", [P, PACK, S], F32)
+        z_pairs = [sbuf("z_pair%d" % i, [P, 2, S], F32) for i in (0, 1)]
         work = [sbuf("work%d" % i, [P, S], F32) for i in range(8)]
-        first = [work[0][:], work[1][:], work[2][:], z[:, 2, :]]
-        lift = [work[3][:], work[4][:], work[5][:], z[:, 3, :]]
-        diff = [work[6][:], work[7][:], first[1], lift[1]]
+        first = [work[0][:], work[1][:], work[2][:], z_pairs[1][:, 0, :]]
+        lift = [work[3][:], work[4][:], work[5][:], z_pairs[1][:, 1, :]]
         absdiff = per_tile("absdiff", S)
         edge = per_tile("edge", S)
-        over = per_tile("over", S)
+        edge_scaled = per_tile("edge_scaled", S)
+        diff = [work[6][:], work[7][:], edge[0][:], edge[1][:]]
+        past = per_tile("past", S)
+        over = [first[1], past[1][:], lift[3], past[3][:]]
         clip = per_tile("clip", S)
         rise = per_tile("rise", S)
 
         def gathered(window, name):
             return window[:].indirect(lists[name][:])
 
-        for t, h in ((0, 0), (1, 0), (1, 1), (2, 0), (3, 0)):
+        for t, h in ((0, 0), (1, 0), (0, 1), (2, 0), (3, 0)):
             cols, bank = y_parts[t][h]
-            nc.scalar.activation(yb[t][:, cols], bank, ACT.Copy, scale=half_gb[:, t : t + 1])
-        cols, bank = y_parts[0][1]
-        nc.vector.tensor_scalar(yb[0][:, cols], bank, half_gb[:, 0:1], None, ALU.mult)
+            nc.scalar.copy(y[t][:, cols], bank)
+        cols, bank = y_parts[1][1]
+        nc.vector.tensor_copy(y[1][:, cols], bank)
 
-        def plain_windows(t):
-            for cols, bank in y_parts[t]:
-                nc.scalar.activation(ya[t][:, cols], bank, ACT.Copy, scale=ga_signed[:, t : t + 1])
-                nc.scalar.copy(y[t][:, cols], bank)
+        gains = sbuf("gains", [P, 2 * PACK], F32)
+        half_gb = sbuf("half_gb", [P, PACK], F32)
+        three_half_gb = sbuf("three_half_gb", [P, PACK], F32)
+        minus_half_gb = sbuf("minus_half_gb", [P, PACK], F32)
+        gb_step = sbuf("gb_step", [P, PACK], F32)
+        gb_sign = sbuf("gb_sign", [P, PACK], F32)
+        ga_signed = sbuf("ga_signed", [P, PACK], F32)
+        nc.tensor.transpose(banks_b[0][:, 0:P], gain_rows[:], ident[:])
+        nc.scalar.copy(gains[:], banks_b[0][:, 0 : 2 * PACK])
+        nc.scalar.activation(half_gb[:], gains[:, PACK:], ACT.Abs, scale=0.5)
+        nc.scalar.activation(three_half_gb[:], gains[:, PACK:], ACT.Abs, scale=1.5)
+        nc.gpsimd.tensor_scalar(gb_step[:], gains[:, PACK:], 0.0, 2.0, ALU.is_ge, ALU.mult)
+        nc.gpsimd.tensor_scalar(gb_sign[:], gb_step[:], 1.0, -1.0, ALU.mult, ALU.add)
+        nc.gpsimd.tensor_tensor(ga_signed[:], gb_sign[:], gains[:, 0:PACK], ALU.mult)
+        nc.gpsimd.tensor_scalar(minus_half_gb[:], half_gb[:], -1.0, 0.0, ALU.mult, ALU.add)
+
+        def gain_window(t):
+            nc.scalar.activation(ya[t][:, 0:S], y[t][:, 0:S], ACT.Copy, scale=ga_signed[:, t : t + 1])
 
         def differences(pair):
             for t in pair:
-                nc.vector.tensor_tensor(diff[t], gathered(yb[t], "n4"), first[t], ALU.subtract)
+                nc.vector.tensor_tensor(diff[t], gathered(y[t], "n4"), first[t], ALU.subtract)
                 nc.scalar.activation(lift[t], diff[t], ACT.Relu)
-                nc.scalar.activation(absdiff[t][:], diff[t], ACT.Abs)
+                nc.scalar.activation(absdiff[t][:], diff[t], ACT.Abs, scale=half_gb[:, t : t + 1])
                 nc.gpsimd.tensor_tensor(edge[t][:], first[t], lift[t], ALU.add)
+            for t in pair:
+                nc.scalar.activation(edge_scaled[t][:], edge[t][:], ACT.Copy, scale=half_gb[:, t : t + 1])
+
+        z_bf = sbuf("z_bf", [P, S * PACK], BF16)
+        z2_turned = z_bf[:].rearrange("j (b u n) -> j b u n", b=4, u=2)
 
         def third(pair):
             for t in pair:
-                nc.vector.tensor_tensor(over[t][:], gathered(yb[t], "n5"), edge[t][:], ALU.subtract)
-                nc.scalar.activation(rise[t][:], over[t][:], ACT.Relu, scale=3.0)
+                nc.vector.tensor_tensor(over[t], gathered(y[t], "n5"), edge[t][:], ALU.subtract)
+                nc.scalar.activation(rise[t][:], over[t], ACT.Relu, scale=three_half_gb[:, t : t + 1])
             for t in pair:
-                nc.vector.scalar_tensor_tensor(clip[t][:], over[t][:], -1.0, absdiff[t][:], ALU.mult, ALU.min)
+                nc.vector.scalar_tensor_tensor(
+                    clip[t][:], over[t], minus_half_gb[:, t : t + 1], absdiff[t][:], ALU.mult, ALU.min
+                )
             for t in pair:
-                for jb in range(4):
-                    cols = slice(P * jb, P * (jb + 1))
-                    for i, term in enumerate((edge, rise, clip)):
+                for i, term in enumerate((edge_scaled, rise, clip)):
+                    for jb in range(4):
+                        cols = slice(P * jb, P * (jb + 1))
                         nc.tensor.matmul(
                             banks_b[jb][:, P * t : P * (t + 1)],
                             term[t][:, cols],
@@ -181,59 +197,56 @@ def tile_picked_selfprodtop2med_none_po_kernel(
                             stop=(i == 2),
                             is_transpose=True,
                         )
+            u = pair[0] // 2
+            for jb in range(4):
+                nc.scalar.copy(
+                    z2_turned[:, jb, u, :].rearrange("j (p e) -> j p e", e=2),
+                    banks_b[jb][:, 2 * P * u : 2 * P * (u + 1)].rearrange("j (e p) -> j p e", e=2),
+                )
+                slot = 2 * (jb % 2) + u
+                nc.tensor.transpose(
+                    banks_a[jb // 2][:, P * slot : P * (slot + 1)], z2_turned[:, jb, u, :].bitcast(F32), ident[:]
+                )
 
-        plain_windows(2)
-        plain_windows(3)
         for t in (0, 1):
-            nc.vector.tensor_copy(first[t], gathered(yb[t], "n3"))
+            nc.vector.tensor_copy(first[t], gathered(y[t], "n3"))
         differences((0, 1))
+        gain_window(2)
+        gain_window(3)
         for t in (2, 3):
-            nc.vector.tensor_copy(first[t], gathered(yb[t], "n3"))
-        plain_windows(0)
-        plain_windows(1)
+            nc.vector.tensor_copy(first[t], gathered(y[t], "n3"))
         third((0, 1))
+        gain_window(0)
+        gain_window(1)
         differences((2, 3))
-        factor = [absdiff[1][:], over[1][:]]
+        factor = [absdiff[1][:], over[1]]
         for t in (2, 3):
             nc.vector.tensor_copy(factor[t % 2], gathered(ya[t], "n1"))
         third((2, 3))
 
-        z2_turned = sbuf("z2_turned", [P, 4, S], BF16)
-        z2_bf = sbuf("z2_bf", [P, S * PACK], BF16)
+        z2_bf = z_pairs[0][:].rearrange("p t j -> p (t j)").bitcast(BF16)
         z2_codes = sbuf("z2_codes", [P, S], U32)
         z2_scales = sbuf("z2_scales", [P, S], U8)
-        for jb in range(4):
+        for h in (0, 1):
             nc.scalar.copy(
-                z2_turned[:, jb, :].rearrange("j (u p e) -> j u p e", u=2, e=2),
-                banks_b[jb][:].rearrange("j (u e p) -> j u p e", u=2, e=2),
+                z_pairs[0][:, h, :].rearrange("p (b j u) -> p b j u", b=2, u=2),
+                banks_a[h][:].rearrange("p (b u j) -> p b j u", b=2, u=2),
             )
-            pairs = z2_turned[:, jb, :].bitcast(F32)
-            for u in (0, 1):
-                slot = 2 * (jb % 2) + u
-                nc.tensor.transpose(
-                    banks_a[jb // 2][:, P * slot : P * (slot + 1)], pairs[:, P * u : P * (u + 1)], ident[:]
-                )
-            if jb % 2 == 1:
-                nc.scalar.copy(
-                    z2_bf[:, 2 * S * (jb // 2) : 2 * S * (jb // 2 + 1)].bitcast(F32).rearrange("p (b j u) -> p b j u", b=2, u=2),
-                    banks_a[jb // 2][:].rearrange("p (b u j) -> p b j u", b=2, u=2),
-                )
 
-        z_bf = sbuf("z_bf", [P, S * PACK], BF16)
         z_codes = sbuf("z_codes", [P, S], U32)
         z_scales = sbuf("z_scales", [P, S], U8)
         z_dst = z_bf[:].rearrange("p (u m t) -> p m u t", u=PACK, t=PACK)
-        z_src = z[:].rearrange("p t (m u) -> p m u t", u=PACK)
+        z_src = [pair[:].rearrange("p t (m u) -> p m u t", u=PACK) for pair in z_pairs]
         for t in (2, 3):
-            nc.vector.tensor_tensor(z[:, t, :], gathered(y[t], "n2"), factor[t % 2], ALU.mult)
-        nc.scalar.copy(z_dst[:, :, :, 2:4], z_src[:, :, :, 2:4])
+            nc.vector.tensor_tensor(z_pairs[t // 2][:, t % 2, :], gathered(y[t], "n2"), factor[t % 2], ALU.mult)
+        nc.scalar.copy(z_dst[:, :, :, 2:4], z_src[1])
         for t in (0, 1):
             nc.vector.tensor_copy(factor[t], gathered(ya[t], "n1"))
-        nc.vector.quantize_mx(out=z2_codes[:].bitcast(FP8X4), scales=z2_scales[:], in_=z2_bf[:])
+        nc.vector.quantize_mx(out=z2_codes[:].bitcast(FP8X4), scales=z2_scales[:], in_=z2_bf)
         for t in (0, 1):
-            nc.vector.tensor_tensor(z[:, t, :], gathered(y[t], "n2"), factor[t], ALU.mult)
-        nc.vector.tensor_copy(z_dst[:, 0:VECTOR_SHARE, :, 0:2], z_src[:, 0:VECTOR_SHARE, :, 0:2])
-        nc.scalar.copy(z_dst[:, VECTOR_SHARE:P, :, 0:2], z_src[:, VECTOR_SHARE:P, :, 0:2])
+            nc.vector.tensor_tensor(z_pairs[t // 2][:, t % 2, :], gathered(y[t], "n2"), factor[t], ALU.mult)
+        nc.vector.tensor_copy(z_dst[:, 0:VECTOR_SHARE, :, 0:2], z_src[0][:, 0:VECTOR_SHARE])
+        nc.scalar.copy(z_dst[:, VECTOR_SHARE:P, :, 0:2], z_src[0][:, VECTOR_SHARE:P])
         s_parts = [[(halves[0], banks_b[0][:, halves[0]]), (halves[1], banks_a[2][:, halves[1]])]]
         s_parts = s_parts + [[(slice(0, S), banks_b[t][:])] for t in (1, 2, 3)]
         for u in range(PACK):
@@ -252,17 +265,18 @@ def tile_picked_selfprodtop2med_none_po_kernel(
                     stop=True,
                 )
 
-        s_window = yb
+        s_window = per_tile("s_window", WINDOW)
         s_plain = work[0:4]
         diff = work[4:8]
         turned = rise
+        over = past
         result = sbuf("result", [P, PACK, S], F32)
         out_rows = out_0.rearrange("(p t) j -> p t j", t=PACK)
         (cols_a, bank_lo), (cols_b, bank_hi) = s_parts[0]
         nc.scalar.activation(s_window[0][:, cols_a], bank_lo, ACT.Copy, scale=0.0625)
         nc.vector.tensor_scalar(s_window[0][:, cols_b], bank_hi, 0.0625, None, ALU.mult)
-        nc.scalar.activation(s_plain[0][:, cols_b], bank_hi, ACT.Copy, scale=0.0625)
-        nc.vector.tensor_scalar(s_plain[0][:, cols_a], bank_lo, 0.0625, None, ALU.mult)
+        nc.scalar.activation(s_plain[0][:, cols_a], bank_lo, ACT.Copy, scale=0.0625)
+        nc.vector.tensor_scalar(s_plain[0][:, cols_b], bank_hi, 0.0625, None, ALU.mult)
         for t in range(1, PACK):
             nc.scalar.activation(s_window[t][:, 0:S], banks_b[t][:], ACT.Copy, scale=0.0625)
             nc.scalar.activation(s_plain[t][:], banks_b[t][:], ACT.Copy, scale=0.0625)
@@ -320,8 +334,8 @@ def tile_picked_selfprodtop2med_none_po_kernel(
                 scales=out_scales[:, cols],
                 in_=out_bf[:, PACK * cols.start : PACK * cols.stop],
             )
-        nc.sync.dma_start(words_out, out_codes[:])
+            nc.sync.dma_start(words_out[:, cols], out_codes[:, cols])
         for q in range(4):
-            nc.scalar.dma_start(
+            (nc.scalar if q < 3 else nc.sync).dma_start(
                 out_2[0, 4 * q : 4 * q + 4, :].bitcast(I32), out_scales[32 * q : 32 * q + 4, :].bitcast(I32)
             )

@@ -103,6 +103,22 @@ def tile_picked_selfprodtop2med_none_po_kernel(
         banks_a = [psum.tile([P, S], F32, name="bank_a%d" % t) for t in range(PACK)]
         banks_b = [psum.tile([P, S], F32, name="bank_b%d" % t) for t in range(PACK)]
 
+        gains = sbuf("gains", [P, 2 * PACK], F32)
+        half_gb = sbuf("half_gb", [P, PACK], F32)
+        three_half_gb = sbuf("three_half_gb", [P, PACK], F32)
+        minus_half_gb = sbuf("minus_half_gb", [P, PACK], F32)
+        gb_step = sbuf("gb_step", [P, PACK], F32)
+        gb_sign = sbuf("gb_sign", [P, PACK], F32)
+        ga_signed = sbuf("ga_signed", [P, PACK], F32)
+        nc.tensor.transpose(banks_b[3][:, 0:P], gain_rows[:], ident[:])
+        nc.scalar.copy(gains[:], banks_b[3][:, 0 : 2 * PACK])
+        nc.scalar.activation(half_gb[:], gains[:, PACK:], ACT.Abs, scale=0.5)
+        nc.scalar.activation(three_half_gb[:], gains[:, PACK:], ACT.Abs, scale=1.5)
+        nc.gpsimd.tensor_scalar(gb_step[:], gains[:, PACK:], 0.0, 2.0, ALU.is_ge, ALU.mult)
+        nc.gpsimd.tensor_scalar(gb_sign[:], gb_step[:], 1.0, -1.0, ALU.mult, ALU.add)
+        nc.gpsimd.tensor_tensor(ga_signed[:], gb_sign[:], gains[:, 0:PACK], ALU.mult)
+        nc.gpsimd.tensor_scalar(minus_half_gb[:], half_gb[:], -1.0, 0.0, ALU.mult, ALU.add)
+
         def first_product(t, cols, bank):
             nc.tensor.matmul_mx(
                 out=bank,
@@ -145,22 +161,6 @@ def tile_picked_selfprodtop2med_none_po_kernel(
             nc.scalar.copy(y[t][:, cols], bank)
         cols, bank = y_parts[1][1]
         nc.vector.tensor_copy(y[1][:, cols], bank)
-
-        gains = sbuf("gains", [P, 2 * PACK], F32)
-        half_gb = sbuf("half_gb", [P, PACK], F32)
-        three_half_gb = sbuf("three_half_gb", [P, PACK], F32)
-        minus_half_gb = sbuf("minus_half_gb", [P, PACK], F32)
-        gb_step = sbuf("gb_step", [P, PACK], F32)
-        gb_sign = sbuf("gb_sign", [P, PACK], F32)
-        ga_signed = sbuf("ga_signed", [P, PACK], F32)
-        nc.tensor.transpose(banks_b[0][:, 0:P], gain_rows[:], ident[:])
-        nc.scalar.copy(gains[:], banks_b[0][:, 0 : 2 * PACK])
-        nc.scalar.activation(half_gb[:], gains[:, PACK:], ACT.Abs, scale=0.5)
-        nc.scalar.activation(three_half_gb[:], gains[:, PACK:], ACT.Abs, scale=1.5)
-        nc.gpsimd.tensor_scalar(gb_step[:], gains[:, PACK:], 0.0, 2.0, ALU.is_ge, ALU.mult)
-        nc.gpsimd.tensor_scalar(gb_sign[:], gb_step[:], 1.0, -1.0, ALU.mult, ALU.add)
-        nc.gpsimd.tensor_tensor(ga_signed[:], gb_sign[:], gains[:, 0:PACK], ALU.mult)
-        nc.gpsimd.tensor_scalar(minus_half_gb[:], half_gb[:], -1.0, 0.0, ALU.mult, ALU.add)
 
         def gain_window(t):
             nc.scalar.activation(ya[t][:, 0:S], y[t][:, 0:S], ACT.Copy, scale=ga_signed[:, t : t + 1])

from contextlib import ExitStack

import concourse.mybir as mybir
from concourse.masks import make_identity

K, T, S, H = 512, 2048, 512, 512
FLOPS = 2 * K * H * S + 2 * H * S * S

F32 = mybir.dt.float32
BF16 = mybir.dt.bfloat16
I32 = mybir.dt.int32
U32 = mybir.dt.uint32
U16 = mybir.dt.uint16
U8 = mybir.dt.uint8
FP8X4 = mybir.dt.float8_e4m3fn_x4
FP4X4 = mybir.dt.float4_e2m1fn_x4
ALU = mybir.AluOpType
ACT = mybir.ActivationFunctionType

P = 128
PACK = 4
WINDOW = 2 * S
VECTOR_SHARE = 88
CLEAR_SPLIT = 768


def tile_picked_selfprodtop2med_none_po_kernel(
    tc, x_words, x_scales, w1_words, w1_scales, ga, gb, offs, n1, n2, n3, n4, n5, n6, n7, out_0, out_1, out_2
):
    nc = tc.nc
    with ExitStack() as ctx:
        keep = ctx.enter_context(tc.tile_pool(name="keep", bufs=1))
        psum = ctx.enter_context(tc.psum_pool(name="psum", bufs=1))

        def sbuf(name, shape, dtype):
            return keep.tile(shape, dtype, name=name, align_bytes=64)

        def per_tile(name, width):
            return [sbuf("%s%d" % (name, t), [P, width], F32) for t in range(PACK)]

        lists = {}
        for name in ("offs", "n1", "n2", "n3", "n4", "n5", "n6", "n7"):
            lists[name] = sbuf(name, [P, S // 16], U16)

        x_table = sbuf("x_table", [P, T], I32)
        x_scale_table = sbuf("x_scale_table", [P, T], U8)
        w_raw = sbuf("w_raw", [P, 2 * H], U8)
        w_scale_raw = sbuf("w_scale_raw", [P, H], U8)
        gain_rows = sbuf("gain_rows", [P, P], F32)

        nc.vector.memset(w_scale_raw[:].bitcast(I32), 0)
        nc.vector.memset(x_scale_table[:, 0:CLEAR_SPLIT].bitcast(I32), 0)
        nc.gpsimd.memset(x_scale_table[:, CLEAR_SPLIT:T].bitcast(I32), 0)
        nc.vector.memset(gain_rows[:], 0.0)

        def load_scale_rows(queue, tile, src, q):
            queue.dma_start(tile[32 * q : 32 * q + 4, :].bitcast(I32), src[0, 4 * q : 4 * q + 4, :].bitcast(I32))

        nc.sync.dma_start(lists["offs"][:], offs)
        nc.sync.dma_start(w_raw[:].bitcast(I32), w1_words[0].bitcast(I32))
        x_rows = x_words[0].rearrange("p n t -> p (n t)").bitcast(I32)
        nc.sync.dma_start(x_table[:, 0 : T // 4], x_rows[:, 0 : T // 4])
        for q in range(4):
            load_scale_rows(nc.sync, x_scale_table, x_scales, q)
        nc.sync.dma_start(x_table[:, T // 4 : T], x_rows[:, T // 4 : T])
        for q in range(4):
            load_scale_rows(nc.sync, w_scale_raw, w1_scales, q)
        nc.sync.dma_start(lists["n3"][:], n3)
        for first_row, gain in ((0, ga), (PACK, gb)):
            nc.sync.dma_start(
                gain_rows[first_row : first_row + PACK, :].rearrange("t (b c) -> t b c", c=8),
                gain.rearrange("(b t c) o -> t b (c o)", t=PACK, c=8),
            )
        for name, src in (("n4", n4), ("n5", n5), ("n1", n1), ("n2", n2), ("n6", n6), ("n7", n7)):
            nc.sync.dma_start(lists[name][:], src)

        ident = sbuf("ident", [P, P], F32)
        make_identity(nc, ident[:])

        w_dealt = sbuf("w_dealt", [P, 2 * H], U8)
        w_scale_dealt = sbuf("w_scale_dealt", [P, H], U8)
        x_picked = sbuf("x_picked", [P, S], I32)
        x_scale_picked = sbuf("x_scale_picked", [P, S], U8)
        nc.vector.tensor_copy(
            w_dealt[:].bitcast(I32).rearrange("p (t b c) -> p b t c", t=PACK, c=4),
            w_raw[:].bitcast(I32).rearrange("p (b t c) -> p b t c", t=PACK, c=4),
        )
        nc.vector.tensor_copy(x_scale_picked[:], x_scale_table[:].indirect(lists["offs"][:]))
        halves = (slice(0, S // 2), slice(S // 2, S))

        def entries(name, cols):
            return lists[name][:, cols.start // 16 : cols.stop // 16]

        nc.gpsimd.tensor_copy(
            w_scale_dealt[:].bitcast(I32).rearrange("p (t b c) -> p b t c", t=PACK, c=2),
            w_scale_raw[:].bitcast(I32).rearrange("p (b t c) -> p b t c", t=PACK, c=2),
        )
        for cols in halves:
            nc.vector.tensor_copy(
                x_picked[:, cols].bitcast(U32), x_table[:].bitcast(U32).indirect(entries("offs", cols))
            )

        banks_a = [psum.tile([P, S], F32, name="bank_a%d" % t) for t in range(PACK)]
        banks_b = [psum.tile([P, S], F32, name="bank_b%d" % t) for t in range(PACK)]

        gains = sbuf("gains", [P, 2 * PACK], F32)
        half_gb = sbuf("half_gb", [P, PACK], F32)
        three_half_gb = sbuf("three_half_gb", [P, PACK], F32)
        minus_half_gb = sbuf("minus_half_gb", [P, PACK], F32)
        gb_step = sbuf("gb_step", [P, PACK], F32)
        gb_sign = sbuf("gb_sign", [P, PACK], F32)
        ga_signed = sbuf("ga_signed", [P, PACK], F32)
        nc.tensor.transpose(banks_b[3][:, 0:P], gain_rows[:], ident[:])
        nc.scalar.copy(gains[:], banks_b[3][:, 0 : 2 * PACK])
        nc.scalar.activation(half_gb[:], gains[:, PACK:], ACT.Abs, scale=0.5)
        nc.scalar.activation(three_half_gb[:], gains[:, PACK:], ACT.Abs, scale=1.5)
        nc.gpsimd.tensor_scalar(gb_step[:], gains[:, PACK:], 0.0, 2.0, ALU.is_ge, ALU.mult)
        nc.gpsimd.tensor_scalar(gb_sign[:], gb_step[:], 1.0, -1.0, ALU.mult, ALU.add)
        nc.gpsimd.tensor_tensor(ga_signed[:], gb_sign[:], gains[:, 0:PACK], ALU.mult)
        nc.gpsimd.tensor_scalar(minus_half_gb[:], half_gb[:], -1.0, 0.0, ALU.mult, ALU.add)

        def first_product(t, cols, bank):
            nc.tensor.matmul_mx(
                out=bank,
                lhsT=w_dealt[:, 2 * P * t : 2 * P * (t + 1)].bitcast(FP4X4),
                lhsT_scale=w_scale_dealt[:, P * t : P * (t + 1)],
                rhs=x_picked[:, cols].bitcast(FP8X4),
                rhs_scale=x_scale_picked[:, cols],
                start=True,
                stop=True,
            )

        y_parts = [[(halves[0], banks_a[t][:, halves[0]]), (halves[1], banks_b[t][:, halves[1]])] for t in (0, 1)]
        y_parts = y_parts + [[(slice(0, S), banks_a[t][:])] for t in (2, 3)]
        for h in (0, 1):
            for t in (0, 1):
                first_product(t, *y_parts[t][h])
        for t in (2, 3):
            first_product(t, *y_parts[t][0])

        ya = per_tile("ya", WINDOW)
        y = per_tile("y", WINDOW)
        z_pairs = [sbuf("z_pair%d" % i, [P, 2, S], F32) for i in (0, 1)]
        work = [sbuf("work%d" % i, [P, S], F32) for i in range(8)]
        first = [work[0][:], work[1][:], work[2][:], z_pairs[1][:, 0, :]]
        lift = [work[3][:], work[4][:], work[5][:], z_pairs[1][:, 1, :]]
        absdiff = per_tile("absdiff", S)
        edge = per_tile("edge", S)
        edge_scaled = per_tile("edge_scaled", S)
        diff = [work[6][:], work[7][:], edge[0][:], edge[1][:]]
        past = per_tile("past", S)
        over = [first[1], past[1][:], lift[3], past[3][:]]
        clip = per_tile("clip", S)
        rise = per_tile("rise", S)

        def gathered(window, name):
            return window[:].indirect(lists[name][:])

        for t, h in ((0, 0), (1, 0), (0, 1), (2, 0), (3, 0)):
            cols, bank = y_parts[t][h]
            nc.scalar.copy(y[t][:, cols], bank)
        cols, bank = y_parts[1][1]
        nc.vector.tensor_copy(y[1][:, cols], bank)

        def gain_window(t):
            nc.scalar.activation(ya[t][:, 0:S], y[t][:, 0:S], ACT.Copy, scale=ga_signed[:, t : t + 1])

        def differences(pair):
            for t in pair:
                nc.vector.tensor_tensor(diff[t], gathered(y[t], "n4"), first[t], ALU.subtract)
                nc.scalar.activation(lift[t], diff[t], ACT.Relu)
                nc.scalar.activation(absdiff[t][:], diff[t], ACT.Abs, scale=half_gb[:, t : t + 1])
                nc.gpsimd.tensor_tensor(edge[t][:], first[t], lift[t], ALU.add)
            for t in pair:
                nc.scalar.activation(edge_scaled[t][:], edge[t][:], ACT.Copy, scale=half_gb[:, t : t + 1])

        z_bf = sbuf("z_bf", [P, S * PACK], BF16)
        z2_turned = z_bf[:].rearrange("j (b u n) -> j b u n", b=4, u=2)

        def third(pair):
            for t in pair:
                nc.vector.tensor_tensor(over[t], gathered(y[t], "n5"), edge[t][:], ALU.subtract)
                nc.scalar.activation(rise[t][:], over[t], ACT.Relu, scale=three_half_gb[:, t : t + 1])
            for t in pair:
                nc.vector.scalar_tensor_tensor(
                    clip[t][:], over[t], minus_half_gb[:, t : t + 1], absdiff[t][:], ALU.mult, ALU.min
                )
            for t in pair:
                for i, term in enumerate((edge_scaled, rise, clip)):
                    for jb in range(4):
                        cols = slice(P * jb, P * (jb + 1))
                        nc.tensor.matmul(
                            banks_b[jb][:, P * t : P * (t + 1)],
                            term[t][:, cols],
                            ident[:],
                            start=(i == 0),
                            stop=(i == 2),
                            is_transpose=True,
                        )
            u = pair[0] // 2
            for jb in range(4):
                nc.scalar.copy(
                    z2_turned[:, jb, u, :].rearrange("j (p e) -> j p e", e=2),
                    banks_b[jb][:, 2 * P * u : 2 * P * (u + 1)].rearrange("j (e p) -> j p e", e=2),
                )
                slot = 2 * (jb % 2) + u
                nc.tensor.transpose(
                    banks_a[jb // 2][:, P * slot : P * (slot + 1)], z2_turned[:, jb, u, :].bitcast(F32), ident[:]
                )

        for t in (0, 1):
            nc.vector.tensor_copy(first[t], gathered(y[t], "n3"))
        differences((0, 1))
        gain_window(2)
        gain_window(3)
        for t in (2, 3):
            nc.vector.tensor_copy(first[t], gathered(y[t], "n3"))
        third((0, 1))
        gain_window(0)
        gain_window(1)
        differences((2, 3))
        factor = [absdiff[1][:], over[1]]
        for t in (2, 3):
            nc.vector.tensor_copy(factor[t % 2], gathered(ya[t], "n1"))
        third((2, 3))

        z2_bf = z_pairs[0][:].rearrange("p t j -> p (t j)").bitcast(BF16)
        z2_codes = sbuf("z2_codes", [P, S], U32)
        z2_scales = sbuf("z2_scales", [P, S], U8)
        for h in (0, 1):
            nc.scalar.copy(
                z_pairs[0][:, h, :].rearrange("p (b j u) -> p b j u", b=2, u=2),
                banks_a[h][:].rearrange("p (b u j) -> p b j u", b=2, u=2),
            )

        z_codes = sbuf("z_codes", [P, S], U32)
        z_scales = sbuf("z_scales", [P, S], U8)
        z_dst = z_bf[:].rearrange("p (u m t) -> p m u t", u=PACK, t=PACK)
        z_src = [pair[:].rearrange("p t (m u) -> p m u t", u=PACK) for pair in z_pairs]
        for t in (2, 3):
            nc.vector.tensor_tensor(z_pairs[t // 2][:, t % 2, :], gathered(y[t], "n2"), factor[t % 2], ALU.mult)
        nc.scalar.copy(z_dst[:, :, :, 2:4], z_src[1])
        for t in (0, 1):
            nc.vector.tensor_copy(factor[t], gathered(ya[t], "n1"))
        nc.vector.quantize_mx(out=z2_codes[:].bitcast(FP8X4), scales=z2_scales[:], in_=z2_bf)
        for t in (0, 1):
            nc.vector.tensor_tensor(z_pairs[t // 2][:, t % 2, :], gathered(y[t], "n2"), factor[t], ALU.mult)
        nc.vector.tensor_copy(z_dst[:, 0:VECTOR_SHARE, :, 0:2], z_src[0][:, 0:VECTOR_SHARE])
        nc.scalar.copy(z_dst[:, VECTOR_SHARE:P, :, 0:2], z_src[0][:, VECTOR_SHARE:P])
        s_parts = [[(halves[0], banks_b[0][:, halves[0]]), (halves[1], banks_a[2][:, halves[1]])]]
        s_parts = s_parts + [[(slice(0, S), banks_b[t][:])] for t in (1, 2, 3)]
        for u in range(PACK):
            rows = slice(P * u, P * (u + 1))
            nc.vector.quantize_mx(
                out=z_codes[:, rows].bitcast(FP8X4), scales=z_scales[:, rows], in_=z_bf[:, S * u : S * (u + 1)]
            )
            for cols, bank in s_parts[u]:
                nc.tensor.matmul_mx(
                    out=bank,
                    lhsT=z_codes[:, rows].bitcast(FP8X4),
                    lhsT_scale=z_scales[:, rows],
                    rhs=z2_codes[:, cols].bitcast(FP8X4),
                    rhs_scale=z2_scales[:, cols],
                    start=True,
                    stop=True,
                )

        s_window = per_tile("s_window", WINDOW)
        s_plain = work[0:4]
        diff = work[4:8]
        turned = rise
        over = past
        result = sbuf("result", [P, PACK, S], F32)
        out_rows = out_0.rearrange("(p t) j -> p t j", t=PACK)
        (cols_a, bank_lo), (cols_b, bank_hi) = s_parts[0]
        nc.scalar.activation(s_window[0][:, cols_a], bank_lo, ACT.Copy, scale=0.0625)
        nc.vector.tensor_scalar(s_window[0][:, cols_b], bank_hi, 0.0625, None, ALU.mult)
        nc.scalar.activation(s_plain[0][:, cols_a], bank_lo, ACT.Copy, scale=0.0625)
        nc.vector.tensor_scalar(s_plain[0][:, cols_b], bank_hi, 0.0625, None, ALU.mult)
        for t in range(1, PACK):
            nc.scalar.activation(s_window[t][:, 0:S], banks_b[t][:], ACT.Copy, scale=0.0625)
            nc.scalar.activation(s_plain[t][:], banks_b[t][:], ACT.Copy, scale=0.0625)

        out_bf = sbuf("out_bf", [P, S * PACK], BF16)
        out_codes = sbuf("out_codes", [P, S], I32)
        out_scales = sbuf("out_scales", [P, S], U8)
        o_dst = out_bf[:].rearrange("p (j t) -> p j t", t=PACK)
        o_src = result[:].rearrange("p t j -> p j t")

        def median_sum(t):
            for jb in range(4):
                cols = slice(P * jb, P * (jb + 1))
                for i, term in enumerate((edge, clip)):
                    nc.tensor.matmul(
                        banks_a[t][:, cols], term[t][:, cols], ident[:], start=(i == 0), stop=(i == 1), is_transpose=True
                    )
            nc.scalar.copy(turned[t][:], banks_a[t][:])
            for jb in range(4):
                cols = slice(P * jb, P * (jb + 1))
                nc.tensor.transpose(banks_a[2 + t][:, cols], turned[t][:, cols], ident[:])
            nc.scalar.copy(result[:, t, :], banks_a[2 + t][:])
            nc.sync.dma_start(out_rows[:, t, :], result[:, t, :])

        for pair in ((0, 1), (2, 3)):
            for t in pair:
                nc.vector.tensor_tensor(diff[t][:], gathered(s_window[t], "n6"), s_plain[t][:], ALU.subtract)
                nc.scalar.activation(absdiff[t][:], diff[t][:], ACT.Abs)
            if pair[0] == 2:
                median_sum(0)
                median_sum(1)
                nc.scalar.copy(o_dst[:, :, 0:2], o_src[:, :, 0:2])
            for t in pair:
                nc.vector.scalar_tensor_tensor(edge[t][:], diff[t][:], 0.0, s_plain[t][:], ALU.min, ALU.add)
            for t in pair:
                nc.vector.tensor_tensor(over[t][:], gathered(s_window[t], "n7"), edge[t][:], ALU.subtract)
            if pair[0] == 0:
                for t in pair:
                    nc.vector.scalar_tensor_tensor(clip[t][:], over[t][:], 0.0, absdiff[t][:], ALU.max, ALU.min)

        nc.vector.scalar_tensor_tensor(clip[2][:], over[2][:], 0.0, absdiff[2][:], ALU.max, ALU.min)
        for cols in halves:
            nc.vector.scalar_tensor_tensor(clip[3][:, cols], over[3][:, cols], 0.0, absdiff[3][:, cols], ALU.max, ALU.min)
        nc.vector.tensor_tensor(result[:, 2, :], edge[2][:], clip[2][:], ALU.add)
        nc.sync.dma_start(out_rows[:, 2, :], result[:, 2, :])
        for cols in halves:
            nc.vector.tensor_tensor(result[:, 3, cols], edge[3][:, cols], clip[3][:, cols], ALU.add)
        nc.sync.dma_start(out_rows[:, 3, :], result[:, 3, :])
        nc.scalar.copy(o_dst[:, halves[0], 2:4], o_src[:, halves[0], 2:4])
        nc.vector.tensor_copy(o_dst[:, halves[1], 2:4], o_src[:, halves[1], 2:4])
        words_out = out_1[0].rearrange("p n t -> p (n t)").bitcast(I32)
        for cols in (halves[1], halves[0]):
            nc.vector.quantize_mx(
                out=out_codes[:, cols].bitcast(FP8X4),
                scales=out_scales[:, cols],
                in_=out_bf[:, PACK * cols.start : PACK * cols.stop],
            )
            nc.sync.dma_start(words_out[:, cols], out_codes[:, cols])
        for q in range(4):
            (nc.scalar if q < 3 else nc.sync).dma_start(
                out_2[0, 4 * q : 4 * q + 4, :].bitcast(I32), out_scales[32 * q : 32 * q + 4, :].bitcast(I32)
            )
